import numpy as np
CORES = [15,47,79,175,207]
N = 5
TK = 1024
NT = N * TK
EPS = 0.01
def setup_inputs(rng):
    x = (rng.standard_normal((N, 128, TK), dtype=np.float32) * (0.5 + np.arange(N, dtype=np.float32).reshape(N, 1, 1) / N) + rng.standard_normal((N, 128, 1), dtype=np.float32))
    return {"x": x}
def setup_inputs_big(rng):
    d = setup_inputs(rng)
    for k in ("x",): d[k] = (d[k].astype(np.float32) * 1024.0).astype(d[k].dtype)
    return d
def setup_inputs_small(rng):
    d = setup_inputs(rng)
    for k in ("x",): d[k] = (d[k].astype(np.float32) * (1 / 1024.0)).astype(d[k].dtype)
    return d
def setup_inputs_apart(rng):
    d = setup_inputs(rng)
    f = (10.0 ** rng.permutation(np.linspace(-1.5, 1.5, N))).astype(np.float32).reshape(N, 1, 1)
    for k in ("x",): d[k] = (d[k].astype(np.float32) * f).astype(d[k].dtype)
    return d
def setup_inputs_mixed(rng):
    d = setup_inputs(rng)
    f = (10.0 ** rng.uniform(-3, 3, (1, 128, 1))).astype(np.float32); shape = rng.integers(3, size=(1, 128, 1))
    for k in ("x",):
        x = d[k].astype(np.float32)
        m = x.mean(axis=(0, 2), keepdims=True); level = m + np.sign(x - m) * np.abs(x - m).mean(axis=(0, 2), keepdims=True) * rng.uniform(0.9, 1.1, x.shape).astype(np.float32)
        other = x * np.where(rng.random(x.shape) < 0.5, 0.1, 1.0).astype(np.float32)
        d[k] = (np.where(shape == 1, level, np.where(shape == 2, other, x)) * f).astype(d[k].dtype)
    return d
def setup_inputs_offset(rng):
    d = setup_inputs(rng)
    x = d["x"]; spread = x.std(axis=(0, 2), keepdims=True)
    d["x"] = (x + spread * rng.uniform(16, 48, (1, 128, 1)) * rng.choice([-1.0, 1.0], (1, 128, 1))).astype(np.float32)
    return d
def reference(x):
    X = x.astype(np.float64)
    mu = X.sum(axis=(0, 2)).reshape(1, 128, 1) / NT
    rs = 1.0 / np.sqrt(((X - mu) ** 2).sum(axis=(0, 2)).reshape(1, 128, 1) / NT + EPS)
    n = (X - mu) * rs
    return {"y": n.astype(np.float32)}

@@ -1,0 +1,148 @@
+from concourse.bass import DstId, RemoteDMATransfer
+from concourse.mybir import AluOpType, AxisListType, ActivationFunctionType
+
+N = 5
+TK = 1024
+NT = N * TK
+EPS = 0.01
+NG = 4
+GW = TK // NG
+G = N * NG
+SLOT = 2 * NG
+
+Q, W, MU, B, V, IV, S, A, TT, C, RR = range(11)
+
+SCRATCH = {
+    "xs": ("sbuf", [128, TK], "float32"),
+    "wk": ("sbuf", [128, TK], "float32"),
+    "land": ("sbuf", [128, N * SLOT], "float32"),
+    "sm": ("sbuf", [128, NG], "float32"),
+    "sc": ("sbuf", [128, 16], "float32"),
+    "tj": ("sbuf", [128, 2 * G], "float32"),
+}
+SEMAPHORES = (["ld%d" % i for i in range(NG)] + ["rd%d" % i for i in range(NG)] + ["nm%d" % i for i in range(NG)]
+              + ["sq%d" % i for i in range(NG)]
+              + ["arr1", "arr2", "sent", "eq", "ew", "emu", "eb", "ev", "eiv", "ec0", "ec1", "es", "et", "ec", "ea", "er",
+                 "yav", "yas", "ybv", "ybs", "st0", "st1"])
+
+A_V, A_END = 160, 256
+B_V = 640
+
+
+def rank_program(g, core, T, topo):
+    rank = T.rank_of(core)
+    if rank is None:
+        return
+    sem = T.sem
+    vec, act, syn = g.vector, g.scalar, g.sync
+    mult, add = AluOpType.mult, AluOpType.add
+    AF = ActivationFunctionType
+    base = rank * SLOT
+
+    def col(k):
+        return T.sc[:, k:k + 1]
+
+    negm_all = T.land[:, 0:N * SLOT:2]
+    m2_all = T.land[:, 1:N * SLOT:2]
+
+    others = [T.cores[(rank + k) % N] for k in range(1, N)]
+    mask = topo.mask(core, others[0])
+    for d in others:
+        assert topo.may_write(core, d)
+        mask &= topo.mask(core, d)
+    n_eng = bin(mask).count("1")
+    ids = []
+    for d in others:
+        rid, pid = topo.addr(d, core)
+        ids.append(DstId(rid=rid, pnc=pid))
+
+    def send(lo, hi, arrive):
+        piece = T.land[:, base + lo:base + hi]
+        g.remote_dma_fused([RemoteDMATransfer(dst_ids=ids, dma_engine_mask=mask, remote_sem=arrive,
+                                              srcs=[piece], dsts=[piece for _ in ids], alu_op=0)],
+                           local_sem=sem.sent)
+
+    for i in range(NG):
+        syn.dma_start(T.xs[:, i * GW:(i + 1) * GW], T.x[:, i * GW:(i + 1) * GW]).then_inc(sem["ld%d" % i], 16)
+
+    for i in range(NG):
+        blk = T.xs[:, i * GW:(i + 1) * GW]
+        negm = T.land[:, base + 2 * i:base + 2 * i + 1]
+        vec.wait_ge(sem["ld%d" % i], 16)
+        vec.tensor_reduce(T.sm[:, i:i + 1], blk, AxisListType.X, add).then_inc(sem["rd%d" % i], 1)
+        vec.wait_ge(sem["rd%d" % i], 1)
+        vec.tensor_scalar(negm, T.sm[:, i:i + 1], -1.0 / GW, None, mult).then_inc(sem["nm%d" % i], 1)
+        act.wait_ge(sem["ld%d" % i], 16)
+        act.wait_ge(sem["nm%d" % i], 1)
+        act.activation(T.wk[:, i * GW:(i + 1) * GW], blk, AF.Square, bias=negm, scale=1.0,
+                       accum_out=T.land[:, base + 2 * i + 1:base + 2 * i + 2]).then_inc(sem["sq%d" % i], 1)
+
+    g.wait_ge(sem.nm0, 1)
+    g.wait_ge(sem.sq0, 1)
+    send(0, 2, sem.arr1)
+    for i in range(1, NG):
+        g.wait_ge(sem["nm%d" % i], 1)
+        g.wait_ge(sem["sq%d" % i], 1)
+    send(2, SLOT, sem.arr2)
+
+    full = (N - 1) * n_eng
+    act.wait_ge(sem.arr1, full)
+    act.wait_ge(sem.arr2, full)
+    act.activation(T.tj[:, 0:G], negm_all, AF.Identity, scale=-1.0 / G, accum_out=col(MU)).then_inc(sem.emu, 1)
+    act.wait_ge(sem.emu, 1)
+    act.activation(T.tj[:, G:2 * G], negm_all, AF.Square, bias=col(MU), scale=1.0,
+                   accum_out=col(B)).then_inc(sem.eb, 1)
+    act.wait_ge(sem.eb, 1)
+    act.wait_ge(sem.ew, 1)
+    act.activation(col(S), col(B), AF.Sqrt, bias=col(W), scale=1.0 / G).then_inc(sem.es, 1)
+
+    for i in range(NG):
+        vec.wait_ge(sem["sq%d" % i], 1)
+    vec.wait_ge(sem.arr1, full)
+    vec.wait_ge(sem.arr2, full)
+    vec.tensor_reduce(col(Q), m2_all, AxisListType.X, add).then_inc(sem.eq, 1)
+    vec.wait_ge(sem.eq, 1)
+    vec.tensor_scalar(col(W), col(Q), 1.0 / NT, EPS, mult, add).then_inc(sem.ew, 1)
+    vec.wait_ge(sem.emu, 1)
+    vec.tensor_scalar(T.wk[:, 0:A_END], T.xs[:, 0:A_END], col(MU), None, AluOpType.subtract).then_inc(sem.ec0, 1)
+    vec.wait_ge(sem.ew, 1)
+    vec.wait_ge(sem.eb, 1)
+    vec.tensor_scalar(col(V), col(B), 1.0 / G, col(W), mult, add).then_inc(sem.ev, 1)
+    vec.wait_ge(sem.ev, 1)
+    vec.reciprocal(col(IV), col(V)).then_inc(sem.eiv, 1)
+    vec.tensor_scalar(T.wk[:, A_END:TK], T.xs[:, A_END:TK], col(MU), None, AluOpType.subtract).then_inc(sem.ec1, 1)
+
+    vec.wait_ge(sem.es, 1)
+    vec.wait_ge(sem.eiv, 1)
+    vec.tensor_scalar(col(TT), col(S), col(S), col(IV), mult, mult).then_inc(sem.et, 1)
+    vec.wait_ge(sem.et, 1)
+    vec.tensor_scalar(col(C), col(TT), -0.5, 1.5, mult, add).then_inc(sem.ec, 1)
+    act.wait_ge(sem.es, 1)
+    act.wait_ge(sem.eiv, 1)
+    act.activation(col(A), col(S), AF.Identity, scale=col(IV)).then_inc(sem.ea, 1)
+    act.wait_ge(sem.ea, 1)
+    act.wait_ge(sem.ec, 1)
+    act.activation(col(RR), col(A), AF.Identity, scale=col(C)).then_inc(sem.er, 1)
+
+    vec.wait_ge(sem.ec, 1)
+    vec.wait_ge(sem.ea, 1)
+    vec.wait_ge(sem.ec0, 1)
+    vec.tensor_scalar(T.wk[:, 0:A_V], T.wk[:, 0:A_V], col(A), col(C), mult, mult).then_inc(sem.yav, 1)
+    vec.wait_ge(sem.ec1, 1)
+    vec.tensor_scalar(T.wk[:, A_END:B_V], T.wk[:, A_END:B_V], col(A), col(C), mult, mult).then_inc(sem.ybv, 1)
+    act.wait_ge(sem.er, 1)
+    act.wait_ge(sem.ec0, 1)
+    act.activation(T.wk[:, A_V:A_END], T.wk[:, A_V:A_END], AF.Identity, scale=col(RR)).then_inc(sem.yas, 1)
+    act.wait_ge(sem.ec1, 1)
+    act.activation(T.wk[:, B_V:TK], T.wk[:, B_V:TK], AF.Identity, scale=col(RR)).then_inc(sem.ybs, 1)
+
+    syn.wait_ge(sem.yav, 1)
+    syn.wait_ge(sem.yas, 1)
+    syn.dma_start(T.y[:, 0:A_END], T.wk[:, 0:A_END]).then_inc(sem.st0, 16)
+    syn.wait_ge(sem.ybv, 1)
+    syn.wait_ge(sem.ybs, 1)
+    syn.dma_start(T.y[:, A_END:TK], T.wk[:, A_END:TK]).then_inc(sem.st1, 16)
+    syn.wait_ge(sem.st0, 16)
+    syn.wait_ge(sem.st1, 16)
+
+    g.wait_ge(sem.sent, 2 * n_eng)

@@ -10,23 +10,21 @@ GW = TK // NG
 G = N * NG
 SLOT = 2 * NG
 
-Q, W, MU, B, V, IV, S, A, TT, C, RR = range(11)
+Q, W, MU, B, V, IV, S, RR = range(8)
 
 SCRATCH = {
     "xs": ("sbuf", [128, TK], "float32"),
     "wk": ("sbuf", [128, TK], "float32"),
     "land": ("sbuf", [128, N * SLOT], "float32"),
-    "sm": ("sbuf", [128, NG], "float32"),
-    "sc": ("sbuf", [128, 16], "float32"),
+    "sc": ("sbuf", [128, 8], "float32"),
     "tj": ("sbuf", [128, 2 * G], "float32"),
 }
-SEMAPHORES = (["ld%d" % i for i in range(NG)] + ["rd%d" % i for i in range(NG)] + ["nm%d" % i for i in range(NG)]
-              + ["sq%d" % i for i in range(NG)]
-              + ["arr1", "arr2", "sent", "eq", "ew", "emu", "eb", "ev", "eiv", "ec0", "ec1", "es", "et", "ec", "ea", "er",
-                 "yav", "yas", "ybv", "ybs", "st0", "st1"])
+SEMAPHORES = (["ld%d" % i for i in range(NG)] + ["nm%d" % i for i in range(NG)] + ["sq%d" % i for i in range(NG)]
+              + ["arr1", "arr2", "sent", "eq", "ew", "emu", "eb", "ev", "eiv", "ed", "es", "er",
+                 "ya", "ybs", "ybv", "st0", "st1"])
 
-A_V, A_END = 160, 256
-B_V = 640
+A_END = 256
+S_END = 544
 
 
 def rank_program(g, core, T, topo):
@@ -35,15 +33,15 @@ def rank_program(g, core, T, topo):
         return
     sem = T.sem
     vec, act, syn = g.vector, g.scalar, g.sync
-    mult, add = AluOpType.mult, AluOpType.add
+    mult, add, sub = AluOpType.mult, AluOpType.add, AluOpType.subtract
     AF = ActivationFunctionType
     base = rank * SLOT
 
     def col(k):
         return T.sc[:, k:k + 1]
 
-    negm_all = T.land[:, 0:N * SLOT:2]
-    m2_all = T.land[:, 1:N * SLOT:2]
+    negs_all = T.land[:, 0:N * SLOT:2]
+    q_all = T.land[:, 1:N * SLOT:2]
 
     others = [T.cores[(rank + k) % N] for k in range(1, N)]
     mask = topo.mask(core, others[0])
@@ -67,14 +65,12 @@ def rank_program(g, core, T, topo):
 
     for i in range(NG):
         blk = T.xs[:, i * GW:(i + 1) * GW]
-        negm = T.land[:, base + 2 * i:base + 2 * i + 1]
+        negs = T.land[:, base + 2 * i:base + 2 * i + 1]
         vec.wait_ge(sem["ld%d" % i], 16)
-        vec.tensor_reduce(T.sm[:, i:i + 1], blk, AxisListType.X, add).then_inc(sem["rd%d" % i], 1)
-        vec.wait_ge(sem["rd%d" % i], 1)
-        vec.tensor_scalar(negm, T.sm[:, i:i + 1], -1.0 / GW, None, mult).then_inc(sem["nm%d" % i], 1)
+        vec.tensor_reduce(negs, blk, AxisListType.X, add, negate=True).then_inc(sem["nm%d" % i], 1)
         act.wait_ge(sem["ld%d" % i], 16)
         act.wait_ge(sem["nm%d" % i], 1)
-        act.activation(T.wk[:, i * GW:(i + 1) * GW], blk, AF.Square, bias=negm, scale=1.0,
+        act.activation(T.wk[:, i * GW:(i + 1) * GW], blk, AF.Square, bias=negs, scale=float(GW),
                        accum_out=T.land[:, base + 2 * i + 1:base + 2 * i + 2]).then_inc(sem["sq%d" % i], 1)
 
     g.wait_ge(sem.nm0, 1)
@@ -88,59 +84,42 @@ def rank_program(g, core, T, topo):
     full = (N - 1) * n_eng
     act.wait_ge(sem.arr1, full)
     act.wait_ge(sem.arr2, full)
-    act.activation(T.tj[:, 0:G], negm_all, AF.Identity, scale=-1.0 / G, accum_out=col(MU)).then_inc(sem.emu, 1)
+    act.activation(T.tj[:, 0:G], negs_all, AF.Identity, scale=-1.0 / NT, accum_out=col(MU)).then_inc(sem.emu, 1)
     act.wait_ge(sem.emu, 1)
-    act.activation(T.tj[:, G:2 * G], negm_all, AF.Square, bias=col(MU), scale=1.0,
+    act.activation(T.tj[:, G:2 * G], negs_all, AF.Square, bias=col(MU), scale=1.0 / GW,
                    accum_out=col(B)).then_inc(sem.eb, 1)
     act.wait_ge(sem.eb, 1)
     act.wait_ge(sem.ew, 1)
     act.activation(col(S), col(B), AF.Sqrt, bias=col(W), scale=1.0 / G).then_inc(sem.es, 1)
+    act.wait_ge(sem.es, 1)
+    act.wait_ge(sem.ed, 1)
+    act.activation(T.wk[:, 0:A_END], T.wk[:, 0:A_END], AF.Identity, scale=col(S)).then_inc(sem.ya, 1)
+    act.activation(T.wk[:, A_END:S_END], T.wk[:, A_END:S_END], AF.Identity, scale=col(S)).then_inc(sem.ybs, 1)
 
     for i in range(NG):
         vec.wait_ge(sem["sq%d" % i], 1)
     vec.wait_ge(sem.arr1, full)
     vec.wait_ge(sem.arr2, full)
-    vec.tensor_reduce(col(Q), m2_all, AxisListType.X, add).then_inc(sem.eq, 1)
+    vec.tensor_reduce(col(Q), q_all, AxisListType.X, add).then_inc(sem.eq, 1)
     vec.wait_ge(sem.eq, 1)
-    vec.tensor_scalar(col(W), col(Q), 1.0 / NT, EPS, mult, add).then_inc(sem.ew, 1)
-    vec.wait_ge(sem.emu, 1)
-    vec.tensor_scalar(T.wk[:, 0:A_END], T.xs[:, 0:A_END], col(MU), None, AluOpType.subtract).then_inc(sem.ec0, 1)
+    vec.tensor_scalar(col(W), col(Q), 1.0 / (float(GW) * GW * NT), EPS, mult, add).then_inc(sem.ew, 1)
     vec.wait_ge(sem.ew, 1)
     vec.wait_ge(sem.eb, 1)
     vec.tensor_scalar(col(V), col(B), 1.0 / G, col(W), mult, add).then_inc(sem.ev, 1)
     vec.wait_ge(sem.ev, 1)
     vec.reciprocal(col(IV), col(V)).then_inc(sem.eiv, 1)
-    vec.tensor_scalar(T.wk[:, A_END:TK], T.xs[:, A_END:TK], col(MU), None, AluOpType.subtract).then_inc(sem.ec1, 1)
-
-    vec.wait_ge(sem.es, 1)
     vec.wait_ge(sem.eiv, 1)
-    vec.tensor_scalar(col(TT), col(S), col(S), col(IV), mult, mult).then_inc(sem.et, 1)
-    vec.wait_ge(sem.et, 1)
-    vec.tensor_scalar(col(C), col(TT), -0.5, 1.5, mult, add).then_inc(sem.ec, 1)
-    act.wait_ge(sem.es, 1)
-    act.wait_ge(sem.eiv, 1)
-    act.activation(col(A), col(S), AF.Identity, scale=col(IV)).then_inc(sem.ea, 1)
-    act.wait_ge(sem.ea, 1)
-    act.wait_ge(sem.ec, 1)
-    act.activation(col(RR), col(A), AF.Identity, scale=col(C)).then_inc(sem.er, 1)
+    vec.wait_ge(sem.emu, 1)
+    vec.tensor_scalar(T.wk[:, 0:S_END], T.xs[:, 0:S_END], col(MU), col(IV), sub, mult).then_inc(sem.ed, 1)
+    vec.wait_ge(sem.es, 1)
+    vec.tensor_scalar(col(RR), col(S), col(IV), None, mult).then_inc(sem.er, 1)
+    vec.wait_ge(sem.er, 1)
+    vec.tensor_scalar(T.wk[:, S_END:TK], T.xs[:, S_END:TK], col(MU), col(RR), sub, mult).then_inc(sem.ybv, 1)
 
-    vec.wait_ge(sem.ec, 1)
-    vec.wait_ge(sem.ea, 1)
-    vec.wait_ge(sem.ec0, 1)
-    vec.tensor_scalar(T.wk[:, 0:A_V], T.wk[:, 0:A_V], col(A), col(C), mult, mult).then_inc(sem.yav, 1)
-    vec.wait_ge(sem.ec1, 1)
-    vec.tensor_scalar(T.wk[:, A_END:B_V], T.wk[:, A_END:B_V], col(A), col(C), mult, mult).then_inc(sem.ybv, 1)
-    act.wait_ge(sem.er, 1)
-    act.wait_ge(sem.ec0, 1)
-    act.activation(T.wk[:, A_V:A_END], T.wk[:, A_V:A_END], AF.Identity, scale=col(RR)).then_inc(sem.yas, 1)
-    act.wait_ge(sem.ec1, 1)
-    act.activation(T.wk[:, B_V:TK], T.wk[:, B_V:TK], AF.Identity, scale=col(RR)).then_inc(sem.ybs, 1)
-
-    syn.wait_ge(sem.yav, 1)
-    syn.wait_ge(sem.yas, 1)
+    syn.wait_ge(sem.ya, 1)
     syn.dma_start(T.y[:, 0:A_END], T.wk[:, 0:A_END]).then_inc(sem.st0, 16)
-    syn.wait_ge(sem.ybv, 1)
     syn.wait_ge(sem.ybs, 1)
+    syn.wait_ge(sem.ybv, 1)
     syn.dma_start(T.y[:, A_END:TK], T.wk[:, A_END:TK]).then_inc(sem.st1, 16)
     syn.wait_ge(sem.st0, 16)
     syn.wait_ge(sem.st1, 16)

@@ -9,22 +9,26 @@ NG = 4
 GW = TK // NG
 G = N * NG
 SLOT = 2 * NG
+LW = N * SLOT
+KQ = 1.0 / (float(GW) * GW * NT)
 
-Q, W, MU, B, V, IV, S, RR = range(8)
+NMU, B, SA, AA, IA, J, J1, RHO, K1, SP, RP, RS = range(12)
 
 SCRATCH = {
     "xs": ("sbuf", [128, TK], "float32"),
     "wk": ("sbuf", [128, TK], "float32"),
-    "land": ("sbuf", [128, N * SLOT], "float32"),
-    "sc": ("sbuf", [128, 8], "float32"),
+    "land": ("sbuf", [128, LW + 4], "float32"),
+    "sc": ("sbuf", [128, 12], "float32"),
     "tj": ("sbuf", [128, 2 * G], "float32"),
+    "d0": ("sbuf", [128, G + 2], "float32"),
+    "scn": ("sbuf", [128, G + 2], "float32"),
 }
 SEMAPHORES = (["ld%d" % i for i in range(NG)] + ["nm%d" % i for i in range(NG)] + ["sq%d" % i for i in range(NG)]
-              + ["arr1", "arr2", "sent", "eq", "ew", "emu", "eb", "ev", "eiv", "ed", "es", "er",
-                 "ya", "ybs", "ybv", "st0", "st1"])
+              + ["arr1", "arr2", "sent", "ms", "esa", "ea", "eia", "ej", "ek", "ew", "emu", "eb", "es", "er", "ers",
+                 "pa", "pb", "ya", "yb", "yc", "st0", "st1"])
 
 A_END = 256
-S_END = 544
+B_END = 512
 
 
 def rank_program(g, core, T, topo):
@@ -33,15 +37,17 @@ def rank_program(g, core, T, topo):
         return
     sem = T.sem
     vec, act, syn = g.vector, g.scalar, g.sync
-    mult, add, sub = AluOpType.mult, AluOpType.add, AluOpType.subtract
+    mult, add = AluOpType.mult, AluOpType.add
     AF = ActivationFunctionType
     base = rank * SLOT
 
     def col(k):
         return T.sc[:, k:k + 1]
 
-    negs_all = T.land[:, 0:N * SLOT:2]
-    q_all = T.land[:, 1:N * SLOT:2]
+    negs_all = T.land[:, 0:LW:2]
+    q_ext = T.land[:, 1:LW + 4:2]
+    q_own = T.land[:, base + SLOT - 3:base + SLOT - 2]
+    wp = T.scn[:, G + 1:G + 2]
 
     others = [T.cores[(rank + k) % N] for k in range(1, N)]
     mask = topo.mask(core, others[0])
@@ -63,6 +69,10 @@ def rank_program(g, core, T, topo):
     for i in range(NG):
         syn.dma_start(T.xs[:, i * GW:(i + 1) * GW], T.x[:, i * GW:(i + 1) * GW]).then_inc(sem["ld%d" % i], 16)
 
+    vec.memset(T.d0[:, 0:G], 1.0).then_inc(sem.ms, 1)
+    vec.memset(T.d0[:, G:G + 1], KQ).then_inc(sem.ms, 1)
+    vec.memset(T.land[:, LW:LW + 4], 0.0).then_inc(sem.ms, 1)
+
     for i in range(NG):
         blk = T.xs[:, i * GW:(i + 1) * GW]
         negs = T.land[:, base + 2 * i:base + 2 * i + 1]
@@ -74,52 +84,69 @@ def rank_program(g, core, T, topo):
                        accum_out=T.land[:, base + 2 * i + 1:base + 2 * i + 2]).then_inc(sem["sq%d" % i], 1)
 
     g.wait_ge(sem.nm0, 1)
-    g.wait_ge(sem.sq0, 1)
-    send(0, 2, sem.arr1)
-    for i in range(1, NG):
+    send(0, 1, sem.arr1)
+    for i in range(NG):
         g.wait_ge(sem["nm%d" % i], 1)
         g.wait_ge(sem["sq%d" % i], 1)
-    send(2, SLOT, sem.arr2)
+    send(1, SLOT, sem.arr2)
+
+    ka = 1.0 / (float(GW) * GW * GW)
+    act.wait_ge(sem["sq%d" % (NG - 2)], 1)
+    act.activation(col(SA), q_own, AF.Sqrt, bias=EPS, scale=ka).then_inc(sem.esa, 1)
+    vec.wait_ge(sem["sq%d" % (NG - 2)], 1)
+    vec.tensor_scalar(col(AA), q_own, ka, EPS, mult, add).then_inc(sem.ea, 1)
+    vec.wait_ge(sem.ea, 1)
+    vec.reciprocal(col(IA), col(AA)).then_inc(sem.eia, 1)
+    vec.wait_ge(sem.eia, 1)
+    vec.tensor_scalar(col(J), col(IA), col(IA), None, mult).then_inc(sem.ej, 1)
+    vec.tensor_scalar(col(J1), col(IA), col(IA), 1.0 / G, mult, mult).then_inc(sem.ej, 1)
+    vec.wait_ge(sem.ej, 2)
+    vec.wait_ge(sem.ms, 3)
+    vec.wait_ge(sem.esa, 1)
+    vec.tensor_scalar(T.d0[:, G + 1:G + 2], col(SA), col(SA), col(J), mult, mult).then_inc(sem.ek, 1)
+    vec.tensor_scalar(col(K1), col(SA), col(SA), col(J1), mult, mult).then_inc(sem.ek, 1)
+    vec.tensor_scalar(col(RHO), col(SA), col(IA), None, mult).then_inc(sem.ek, 1)
 
     full = (N - 1) * n_eng
+    for i in range(NG):
+        act.wait_ge(sem["sq%d" % i], 1)
     act.wait_ge(sem.arr1, full)
     act.wait_ge(sem.arr2, full)
-    act.activation(T.tj[:, 0:G], negs_all, AF.Identity, scale=-1.0 / NT, accum_out=col(MU)).then_inc(sem.emu, 1)
+    act.activation(T.tj[:, 0:G], negs_all, AF.Identity, scale=1.0 / NT, accum_out=col(NMU)).then_inc(sem.emu, 1)
     act.wait_ge(sem.emu, 1)
-    act.activation(T.tj[:, G:2 * G], negs_all, AF.Square, bias=col(MU), scale=1.0 / GW,
+    act.activation(T.tj[:, G:2 * G], negs_all, AF.Square, bias=col(NMU), scale=-1.0 / GW,
                    accum_out=col(B)).then_inc(sem.eb, 1)
     act.wait_ge(sem.eb, 1)
+    act.wait_ge(sem.ek, 3)
     act.wait_ge(sem.ew, 1)
-    act.activation(col(S), col(B), AF.Sqrt, bias=col(W), scale=1.0 / G).then_inc(sem.es, 1)
-    act.wait_ge(sem.es, 1)
-    act.wait_ge(sem.ed, 1)
-    act.activation(T.wk[:, 0:A_END], T.wk[:, 0:A_END], AF.Identity, scale=col(S)).then_inc(sem.ya, 1)
-    act.activation(T.wk[:, A_END:S_END], T.wk[:, A_END:S_END], AF.Identity, scale=col(S)).then_inc(sem.ybs, 1)
+    act.activation(col(SP), col(B), AF.Sqrt, bias=wp, scale=col(K1)).then_inc(sem.es, 1)
+    act.activation(T.wk[:, 0:A_END], T.xs[:, 0:A_END], AF.Identity, bias=col(NMU)).then_inc(sem.pa, 1)
+    act.wait_ge(sem.er, 1)
+    act.activation(col(RS), col(RP), AF.Identity, scale=col(RHO)).then_inc(sem.ers, 1)
+    act.activation(T.wk[:, A_END:B_END], T.xs[:, A_END:B_END], AF.Identity, bias=col(NMU)).then_inc(sem.pb, 1)
+    act.wait_ge(sem.ers, 1)
+    act.wait_ge(sem.pb, 1)
+    act.activation(T.wk[:, A_END:B_END], T.wk[:, A_END:B_END], AF.Identity, scale=col(RS)).then_inc(sem.yb, 1)
 
+    vec.wait_ge(sem.ek, 3)
     for i in range(NG):
         vec.wait_ge(sem["sq%d" % i], 1)
     vec.wait_ge(sem.arr1, full)
     vec.wait_ge(sem.arr2, full)
-    vec.tensor_reduce(col(Q), q_all, AxisListType.X, add).then_inc(sem.eq, 1)
-    vec.wait_ge(sem.eq, 1)
-    vec.tensor_scalar(col(W), col(Q), 1.0 / (float(GW) * GW * NT), EPS, mult, add).then_inc(sem.ew, 1)
-    vec.wait_ge(sem.ew, 1)
-    vec.wait_ge(sem.eb, 1)
-    vec.tensor_scalar(col(V), col(B), 1.0 / G, col(W), mult, add).then_inc(sem.ev, 1)
-    vec.wait_ge(sem.ev, 1)
-    vec.reciprocal(col(IV), col(V)).then_inc(sem.eiv, 1)
-    vec.wait_ge(sem.eiv, 1)
-    vec.wait_ge(sem.emu, 1)
-    vec.tensor_scalar(T.wk[:, 0:S_END], T.xs[:, 0:S_END], col(MU), col(IV), sub, mult).then_inc(sem.ed, 1)
+    vec.tensor_tensor_scan(T.scn[:, 0:G + 2], T.d0[:, 0:G + 2], q_ext, EPS / KQ, mult, add).then_inc(sem.ew, 1)
     vec.wait_ge(sem.es, 1)
-    vec.tensor_scalar(col(RR), col(S), col(IV), None, mult).then_inc(sem.er, 1)
+    vec.reciprocal(col(RP), col(SP)).then_inc(sem.er, 1)
     vec.wait_ge(sem.er, 1)
-    vec.tensor_scalar(T.wk[:, S_END:TK], T.xs[:, S_END:TK], col(MU), col(RR), sub, mult).then_inc(sem.ybv, 1)
+    vec.wait_ge(sem.pa, 1)
+    vec.tensor_scalar(T.wk[:, 0:A_END], T.wk[:, 0:A_END], col(RP), col(RHO), mult, mult).then_inc(sem.ya, 1)
+    vec.wait_ge(sem.emu, 1)
+    vec.wait_ge(sem.ers, 1)
+    vec.tensor_scalar(T.wk[:, B_END:TK], T.xs[:, B_END:TK], col(NMU), col(RS), add, mult).then_inc(sem.yc, 1)
 
     syn.wait_ge(sem.ya, 1)
     syn.dma_start(T.y[:, 0:A_END], T.wk[:, 0:A_END]).then_inc(sem.st0, 16)
-    syn.wait_ge(sem.ybs, 1)
-    syn.wait_ge(sem.ybv, 1)
+    syn.wait_ge(sem.yb, 1)
+    syn.wait_ge(sem.yc, 1)
     syn.dma_start(T.y[:, A_END:TK], T.wk[:, A_END:TK]).then_inc(sem.st1, 16)
     syn.wait_ge(sem.st0, 16)
     syn.wait_ge(sem.st1, 16)

from concourse.bass import DstId, RemoteDMATransfer
from concourse.mybir import AluOpType, AxisListType, ActivationFunctionType

N = 5
TK = 1024
NT = N * TK
EPS = 0.01
NG = 4
GW = TK // NG
G = N * NG
SLOT = 2 * NG
LW = N * SLOT
KQ = 1.0 / (float(GW) * GW * NT)

NMU, B, SA, AA, IA, J, J1, RHO, K1, SP, RP, RS = range(12)

SCRATCH = {
    "xs": ("sbuf", [128, TK], "float32"),
    "wk": ("sbuf", [128, TK], "float32"),
    "land": ("sbuf", [128, LW + 4], "float32"),
    "sc": ("sbuf", [128, 12], "float32"),
    "tj": ("sbuf", [128, 2 * G], "float32"),
    "d0": ("sbuf", [128, G + 2], "float32"),
    "scn": ("sbuf", [128, G + 2], "float32"),
}
SEMAPHORES = (["ld%d" % i for i in range(NG)] + ["nm%d" % i for i in range(NG)] + ["sq%d" % i for i in range(NG)]
              + ["arr1", "arr2", "sent", "ms", "esa", "ea", "eia", "ej", "ek", "ew", "emu", "eb", "es", "er", "ers",
                 "pa", "pb", "ya", "yb", "yc", "st0", "st1"])

A_END = 256
B_END = 512


def rank_program(g, core, T, topo):
    rank = T.rank_of(core)
    if rank is None:
        return
    sem = T.sem
    vec, act, syn = g.vector, g.scalar, g.sync
    mult, add = AluOpType.mult, AluOpType.add
    AF = ActivationFunctionType
    base = rank * SLOT

    def col(k):
        return T.sc[:, k:k + 1]

    negs_all = T.land[:, 0:LW:2]
    q_ext = T.land[:, 1:LW + 4:2]
    q_own = T.land[:, base + SLOT - 3:base + SLOT - 2]
    wp = T.scn[:, G + 1:G + 2]

    others = [T.cores[(rank + k) % N] for k in range(1, N)]
    mask = topo.mask(core, others[0])
    for d in others:
        assert topo.may_write(core, d)
        mask &= topo.mask(core, d)
    n_eng = bin(mask).count("1")
    ids = []
    for d in others:
        rid, pid = topo.addr(d, core)
        ids.append(DstId(rid=rid, pnc=pid))

    def send(lo, hi, arrive):
        piece = T.land[:, base + lo:base + hi]
        g.remote_dma_fused([RemoteDMATransfer(dst_ids=ids, dma_engine_mask=mask, remote_sem=arrive,
                                              srcs=[piece], dsts=[piece for _ in ids], alu_op=0)],
                           local_sem=sem.sent)

    for i in range(NG):
        syn.dma_start(T.xs[:, i * GW:(i + 1) * GW], T.x[:, i * GW:(i + 1) * GW]).then_inc(sem["ld%d" % i], 16)

    vec.memset(T.d0[:, 0:G], 1.0).then_inc(sem.ms, 1)
    vec.memset(T.d0[:, G:G + 1], KQ).then_inc(sem.ms, 1)
    vec.memset(T.land[:, LW:LW + 4], 0.0).then_inc(sem.ms, 1)

    for i in range(NG):
        blk = T.xs[:, i * GW:(i + 1) * GW]
        negs = T.land[:, base + 2 * i:base + 2 * i + 1]
        vec.wait_ge(sem["ld%d" % i], 16)
        vec.tensor_reduce(negs, blk, AxisListType.X, add, negate=True).then_inc(sem["nm%d" % i], 1)
        act.wait_ge(sem["ld%d" % i], 16)
        act.wait_ge(sem["nm%d" % i], 1)
        act.activation(T.wk[:, i * GW:(i + 1) * GW], blk, AF.Square, bias=negs, scale=float(GW),
                       accum_out=T.land[:, base + 2 * i + 1:base + 2 * i + 2]).then_inc(sem["sq%d" % i], 1)

    g.wait_ge(sem.nm0, 1)
    send(0, 1, sem.arr1)
    for i in range(NG):
        g.wait_ge(sem["nm%d" % i], 1)
        g.wait_ge(sem["sq%d" % i], 1)
    send(1, SLOT, sem.arr2)

    ka = 1.0 / (float(GW) * GW * GW)
    act.wait_ge(sem["sq%d" % (NG - 2)], 1)
    act.activation(col(SA), q_own, AF.Sqrt, bias=EPS, scale=ka).then_inc(sem.esa, 1)
    vec.wait_ge(sem["sq%d" % (NG - 2)], 1)
    vec.tensor_scalar(col(AA), q_own, ka, EPS, mult, add).then_inc(sem.ea, 1)
    vec.wait_ge(sem.ea, 1)
    vec.reciprocal(col(IA), col(AA)).then_inc(sem.eia, 1)
    vec.wait_ge(sem.eia, 1)
    vec.tensor_scalar(col(J), col(IA), col(IA), None, mult).then_inc(sem.ej, 1)
    vec.tensor_scalar(col(J1), col(IA), col(IA), 1.0 / G, mult, mult).then_inc(sem.ej, 1)
    vec.wait_ge(sem.ej, 2)
    vec.wait_ge(sem.ms, 3)
    vec.wait_ge(sem.esa, 1)
    vec.tensor_scalar(T.d0[:, G + 1:G + 2], col(SA), col(SA), col(J), mult, mult).then_inc(sem.ek, 1)
    vec.tensor_scalar(col(K1), col(SA), col(SA), col(J1), mult, mult).then_inc(sem.ek, 1)
    vec.tensor_scalar(col(RHO), col(SA), col(IA), None, mult).then_inc(sem.ek, 1)

    full = (N - 1) * n_eng
    for i in range(NG):
        act.wait_ge(sem["sq%d" % i], 1)
    act.wait_ge(sem.arr1, full)
    act.wait_ge(sem.arr2, full)
    act.activation(T.tj[:, 0:G], negs_all, AF.Identity, scale=1.0 / NT, accum_out=col(NMU)).then_inc(sem.emu, 1)
    act.wait_ge(sem.emu, 1)
    act.activation(T.tj[:, G:2 * G], negs_all, AF.Square, bias=col(NMU), scale=-1.0 / GW,
                   accum_out=col(B)).then_inc(sem.eb, 1)
    act.wait_ge(sem.eb, 1)
    act.wait_ge(sem.ek, 3)
    act.wait_ge(sem.ew, 1)
    act.activation(col(SP), col(B), AF.Sqrt, bias=wp, scale=col(K1)).then_inc(sem.es, 1)
    act.activation(T.wk[:, 0:A_END], T.xs[:, 0:A_END], AF.Identity, bias=col(NMU)).then_inc(sem.pa, 1)
    act.wait_ge(sem.er, 1)
    act.activation(col(RS), col(RP), AF.Identity, scale=col(RHO)).then_inc(sem.ers, 1)
    act.activation(T.wk[:, A_END:B_END], T.xs[:, A_END:B_END], AF.Identity, bias=col(NMU)).then_inc(sem.pb, 1)
    act.wait_ge(sem.ers, 1)
    act.wait_ge(sem.pb, 1)
    act.activation(T.wk[:, A_END:B_END], T.wk[:, A_END:B_END], AF.Identity, scale=col(RS)).then_inc(sem.yb, 1)

    vec.wait_ge(sem.ek, 3)
    for i in range(NG):
        vec.wait_ge(sem["sq%d" % i], 1)
    vec.wait_ge(sem.arr1, full)
    vec.wait_ge(sem.arr2, full)
    vec.tensor_tensor_scan(T.scn[:, 0:G + 2], T.d0[:, 0:G + 2], q_ext, EPS / KQ, mult, add).then_inc(sem.ew, 1)
    vec.wait_ge(sem.es, 1)
    vec.reciprocal(col(RP), col(SP)).then_inc(sem.er, 1)
    vec.wait_ge(sem.er, 1)
    vec.wait_ge(sem.pa, 1)
    vec.tensor_scalar(T.wk[:, 0:A_END], T.wk[:, 0:A_END], col(RP), col(RHO), mult, mult).then_inc(sem.ya, 1)
    vec.wait_ge(sem.emu, 1)
    vec.wait_ge(sem.ers, 1)
    vec.tensor_scalar(T.wk[:, B_END:TK], T.xs[:, B_END:TK], col(NMU), col(RS), add, mult).then_inc(sem.yc, 1)

    syn.wait_ge(sem.ya, 1)
    syn.dma_start(T.y[:, 0:A_END], T.wk[:, 0:A_END]).then_inc(sem.st0, 16)
    syn.wait_ge(sem.yb, 1)
    syn.wait_ge(sem.yc, 1)
    syn.dma_start(T.y[:, A_END:TK], T.wk[:, A_END:TK]).then_inc(sem.st1, 16)
    syn.wait_ge(sem.st0, 16)
    syn.wait_ge(sem.st1, 16)

    g.wait_ge(sem.sent, 2 * n_eng)
